import numpy as np
import ml_dtypes


def mxq(x, axis, fmt="e4m3"):
    dtype, down = {"e4m3": (ml_dtypes.float8_e4m3fn, 7), "e5m2": (ml_dtypes.float8_e5m2, 14)}[fmt]
    v = np.moveaxis(np.asarray(x, np.float32).astype(ml_dtypes.bfloat16).astype(np.float64), axis, -1)
    blocks = v.reshape(v.shape[:-1] + (-1, 32))
    amax = np.abs(blocks).max(-1, keepdims=True)
    byte = np.maximum(np.where(amax > 0, np.frexp(amax)[1] - 1 + 127, 0) - down, 1)
    scale = np.exp2(byte - 127.0)
    codes = (blocks / scale).astype(np.float32).astype(dtype).astype(np.float64)
    return np.moveaxis((codes * scale).reshape(v.shape), -1, axis)


WIDE = False


def mx_kscale(k):
    if not WIDE:
        return np.ones(k)
    levels = np.array([10, -10, 5, -5, 0])
    if k % 512:
        return np.exp2(np.random.permutation(np.resize(levels, k // 32))).repeat(32)
    a = np.empty((k // 512, 16))
    for p in range(k // 512):
        a[p, :8] = np.random.permutation(np.resize(levels, 8))
        for g in range(8):
            far = levels[np.abs(levels - a[p, g]) >= 10]
            a[p, g + 8] = far[np.random.randint(len(far))]
    return np.exp2(a.ravel()).repeat(32)


def f64(x):
    return np.asarray(x).astype(np.float64)


def striped8(idx):
    return np.asarray(idx).reshape(8, -1, 16).transpose(0, 2, 1).reshape(128, -1).astype(np.uint16)


def unstriped8(offs):
    return offs.reshape(8, 16, -1).transpose(0, 2, 1).reshape(8, -1).astype(np.int64)


def pick8(x, idx, run):
    r = np.arange(len(x))
    return x[r[:, None], idx[r % (8 * run) // run]]


E2M1 = np.array([0.0, 0.5, 1.0, 1.5, 2.0, 3.0, 4.0, 6.0, -0.0, -0.5, -1.0, -1.5, -2.0, -3.0, -4.0, -6.0])


def pack_weight(w, fmt):
    k, n = w.shape
    w = f64(np.asarray(w, np.float32).astype(ml_dtypes.bfloat16)).reshape(k // 32, 32, n)
    amax = np.abs(w).max(1)
    if fmt == "e4m3":
        byte = np.frexp(amax)[1] - 1 + 127 - 7
    else:
        mant, ex = np.frexp(amax / 6.0)
        byte = np.where(mant > 0.5, ex, ex - 1) + 127
    byte = np.clip(np.where(amax > 0, byte, 1), 1, 254)
    scaled = (w * np.exp2(127.0 - byte)[:, None, :]).reshape(k, n).astype(np.float32)
    by_word = np.ascontiguousarray(scaled.reshape(k // 512, 128, 4, n).transpose(0, 1, 3, 2))
    if fmt == "e4m3":
        words = by_word.astype(ml_dtypes.float8_e4m3fn).view(np.uint8)
    else:
        c = by_word.astype(ml_dtypes.float4_e2m1fn).view(np.uint8) & 0xF
        words = (c[..., 0::2] | (c[..., 1::2] << 4)).reshape(k // 512, 128, 2 * n)
    return np.ascontiguousarray(words), np.ascontiguousarray(byte.astype(np.uint8).reshape(k // 512, 16, n))


def unpack_weight(words, scales, fmt):
    g, _, n = scales.shape
    words = np.ascontiguousarray(words).reshape(g, 128, n, -1)
    if fmt == "e4m3":
        vals = words.view(ml_dtypes.float8_e4m3fn).astype(np.float64)
    else:
        nib = np.empty((g, 128, n, 4), np.uint8)
        nib[..., 0::2] = words & 0xF
        nib[..., 1::2] = words >> 4
        vals = E2M1[nib]
    vals = vals * np.repeat(np.exp2(scales.astype(np.float64) - 127.0), 8, axis=1)[..., None]
    return vals.transpose(0, 1, 3, 2).reshape(g * 512, n)


D, T, I, Q = 512, 1024, 512, 128


def setup_inputs():
    n = np.random.standard_normal
    idx = np.stack([np.random.permutation(T)[:I] for _ in range(8)])
    idx2 = np.stack([np.random.permutation(T)[:I] for _ in range(8)])
    idx3 = np.stack([np.random.permutation(T)[:I] for _ in range(8)])
    fd = mx_kscale(D)
    keysp = pack_weight(n((D, T)) / fd[:, None], "e2m1")
    return {
        "query": (n((D, Q)) * 1.0 / np.sqrt(D) * fd[:, None]).astype(np.float32),
        "keys_words": keysp[0],
        "keys_scales": keysp[1],
        "old": (1.0 * n((Q, T))).astype(np.float32),
        "offs": striped8(idx),
        "offs2": striped8(idx2),
        "offs3": striped8(idx3),
    }


def reference(query, keys_words, keys_scales, old, offs, offs2, offs3):
    idx = unstriped8(offs)
    idx2 = unstriped8(offs2)
    idx3 = unstriped8(offs3)
    keysu = unpack_weight(keys_words, keys_scales, "e2m1")
    queryq = mxq(f64(query), 0, "e4m3")
    a = queryq.T @ keysu
    w = pick8(a, idx, 16) - pick8(a, idx2, 16)
    f1 = np.zeros((Q, T))
    f1[np.arange(Q)[:, None], idx[np.arange(Q) % 128 // 16]] = w
    f2 = f1 + f64(old)
    y = pick8(f2, idx3, 16) * w
    return y

@@ -1,0 +1,108 @@
+from contextlib import ExitStack
+
+import concourse.mybir as mybir
+
+D, T, I, Q = 512, 1024, 512, 128
+FLOPS = 2 * D * T * Q
+
+F32 = mybir.dt.float32
+BF16 = mybir.dt.bfloat16
+I32 = mybir.dt.int32
+U32 = mybir.dt.uint32
+U16 = mybir.dt.uint16
+U8 = mybir.dt.uint8
+FP8X4 = mybir.dt.float8_e4m3fn_x4
+FP4X4 = mybir.dt.float4_e2m1fn_x4
+ADD = mybir.AluOpType.add
+MULT = mybir.AluOpType.mult
+COPY = mybir.ActivationFunctionType.Copy
+
+P = 128
+PACK = 4
+N_TILE = 256
+HALF = I // 2
+LIST_COLS = I // 16
+HALF_COLS = LIST_COLS // 2
+
+
+def tile_attend_difference_lean_throughtimes_heads_kernel(tc, query, keys_words, keys_scales, old, offs, offs2, offs3, out):
+    nc = tc.nc
+    with ExitStack() as ctx:
+        sb = ctx.enter_context(tc.tile_pool(name="sb", bufs=1))
+        psum = ctx.enter_context(tc.psum_pool(name="psum", bufs=1))
+
+        list1 = sb.tile([P, LIST_COLS], U16, name="list1")
+        list2 = sb.tile([P, LIST_COLS], U16, name="list2")
+        list3 = sb.tile([P, LIST_COLS], U16, name="list3")
+        q_raw = sb.tile([P, PACK, Q], F32, name="q_raw", align_bytes=64)
+        k_words = sb.tile([P, 2 * T], U8, name="k_words", align_bytes=64)
+        k_scales = sb.tile([P, T], U8, name="k_scales", align_bytes=64)
+        old_sb = sb.tile([P, T], F32, name="old_sb")
+        f1 = sb.tile([P, T], F32, name="f1")
+
+        nc.vector.memset(k_scales[:].bitcast(U32), 0)
+        nc.sync.dma_start(out=q_raw[:], in_=query.rearrange("(p j) q -> p j q", j=PACK))
+        nc.sync.dma_start(out=k_words[:].bitcast(I32), in_=keys_words[0].bitcast(I32))
+        for quad in range(4):
+            nc.scalar.dma_start(
+                out=k_scales[32 * quad : 32 * quad + 4, :].bitcast(I32),
+                in_=keys_scales[0, 4 * quad : 4 * quad + 4, :].bitcast(I32),
+            )
+        nc.sync.dma_start(list1[:], offs)
+        nc.sync.dma_start(list2[:], offs2)
+        nc.sync.dma_start(list3[:], offs3)
+        nc.sync.dma_start(out=old_sb[:], in_=old)
+        nc.vector.memset(f1[:], 0.0)
+
+        q_bf = sb.tile([P, Q, PACK], BF16, name="q_bf", align_bytes=64)
+        nc.vector.tensor_copy(
+            out=q_bf[:].rearrange("p (c i) t -> p c t i", i=4),
+            in_=q_raw[:].rearrange("p t (c i) -> p c t i", i=4),
+        )
+        q_codes = sb.tile([P, Q], U32, name="q_codes", align_bytes=64)
+        q_scales = sb.tile([P, Q], U8, name="q_scales", align_bytes=64)
+        nc.vector.quantize_mx(
+            out=q_codes[:].bitcast(FP8X4), scales=q_scales[:], in_=q_bf[:].rearrange("p q t -> p (q t)")
+        )
+
+        a = sb.tile([P, T], F32, name="a")
+        for n in range(T // N_TILE):
+            cols = slice(n * N_TILE, (n + 1) * N_TILE)
+            bank = psum.tile([P, N_TILE], F32, name="bank%d" % n)
+            nc.tensor.matmul_mx(
+                out=bank[:],
+                lhsT=q_codes[:].bitcast(FP8X4),
+                lhsT_scale=q_scales[:],
+                rhs=k_words[:, 2 * n * N_TILE : 2 * (n + 1) * N_TILE].bitcast(FP4X4),
+                rhs_scale=k_scales[:, cols],
+                start=True,
+                stop=True,
+            )
+            if n % 2 == 0:
+                nc.scalar.activation(a[:, cols], bank[:], COPY)
+            else:
+                nc.vector.tensor_copy(a[:, cols], bank[:])
+
+        halves = [slice(h * HALF_COLS, (h + 1) * HALF_COLS) for h in range(2)]
+        plus = [sb.tile([P, HALF], F32, name="plus%d" % h) for h in range(2)]
+        minus = [sb.tile([P, HALF], F32, name="minus%d" % h) for h in range(2)]
+        w = [sb.tile([P, HALF], F32, name="w%d" % h) for h in range(2)]
+
+        nc.vector.tensor_copy(plus[0][:], a[:].indirect(list1[:, halves[0]]))
+        nc.scalar.activation(minus[0][:], a[:].indirect(list2[:, halves[0]]), COPY, scale=-1.0)
+        nc.scalar.activation(plus[1][:], a[:].indirect(list1[:, halves[1]]), COPY)
+        nc.scalar.activation(minus[1][:], a[:].indirect(list2[:, halves[1]]), COPY, scale=-1.0)
+        for h in range(2):
+            nc.vector.tensor_tensor(f1[:].indirect(list1[:, halves[h]]), plus[h][:], minus[h][:], ADD)
+            nc.vector.tensor_tensor(w[h][:], plus[h][:], minus[h][:], ADD)
+
+        f2 = sb.tile([P, T], F32, name="f2")
+        nc.vector.tensor_tensor(f2[:], f1[:], old_sb[:], ADD)
+
+        picked = sb.tile([P, HALF], F32, name="picked")
+        y = [sb.tile([P, HALF], F32, name="y%d" % h) for h in range(2)]
+        nc.scalar.activation(picked[:], f2[:].indirect(list3[:, halves[1]]), COPY)
+        nc.vector.tensor_tensor(y[0][:], f2[:].indirect(list3[:, halves[0]]), w[0][:], MULT)
+        nc.sync.dma_start(out=out[:, :HALF], in_=y[0][:])
+        nc.vector.tensor_tensor(y[1][:], picked[:], w[1][:], MULT)
+        nc.scalar.dma_start(out=out[:, HALF:], in_=y[1][:])

@@ -19,7 +19,7 @@ COPY = mybir.ActivationFunctionType.Copy
 
 P = 128
 PACK = 4
-N_TILE = 256
+WIDTHS = (256, 256, 256, 128, 128)
 HALF = I // 2
 LIST_COLS = I // 16
 HALF_COLS = LIST_COLS // 2
@@ -34,46 +34,53 @@ def tile_attend_difference_lean_throughtimes_heads_kernel(tc, query, keys_words,
         list1 = sb.tile([P, LIST_COLS], U16, name="list1")
         list2 = sb.tile([P, LIST_COLS], U16, name="list2")
         list3 = sb.tile([P, LIST_COLS], U16, name="list3")
-        q_raw = sb.tile([P, PACK, Q], F32, name="q_raw", align_bytes=64)
+        q_raw = sb.tile([P, PACK, Q], F32, name="q_raw", tag="staged", align_bytes=64)
         k_words = sb.tile([P, 2 * T], U8, name="k_words", align_bytes=64)
         k_scales = sb.tile([P, T], U8, name="k_scales", align_bytes=64)
-        old_sb = sb.tile([P, T], F32, name="old_sb")
         f1 = sb.tile([P, T], F32, name="f1")
 
         nc.vector.memset(k_scales[:].bitcast(U32), 0)
         nc.sync.dma_start(out=q_raw[:], in_=query.rearrange("(p j) q -> p j q", j=PACK))
         nc.sync.dma_start(out=k_words[:].bitcast(I32), in_=keys_words[0].bitcast(I32))
         for quad in range(4):
-            nc.scalar.dma_start(
+            (nc.sync if quad < 2 else nc.scalar).dma_start(
                 out=k_scales[32 * quad : 32 * quad + 4, :].bitcast(I32),
                 in_=keys_scales[0, 4 * quad : 4 * quad + 4, :].bitcast(I32),
             )
         nc.sync.dma_start(list1[:], offs)
         nc.sync.dma_start(list2[:], offs2)
         nc.sync.dma_start(list3[:], offs3)
-        nc.sync.dma_start(out=old_sb[:], in_=old)
         nc.vector.memset(f1[:], 0.0)
 
         q_bf = sb.tile([P, Q, PACK], BF16, name="q_bf", align_bytes=64)
-        nc.vector.tensor_copy(
-            out=q_bf[:].rearrange("p (c i) t -> p c t i", i=4),
-            in_=q_raw[:].rearrange("p t (c i) -> p c t i", i=4),
-        )
         q_codes = sb.tile([P, Q], U32, name="q_codes", align_bytes=64)
         q_scales = sb.tile([P, Q], U8, name="q_scales", align_bytes=64)
-        nc.vector.quantize_mx(
-            out=q_codes[:].bitcast(FP8X4), scales=q_scales[:], in_=q_bf[:].rearrange("p q t -> p (q t)")
-        )
+        q_halves = [slice(0, Q // 2), slice(Q // 2, Q)]
+        for rows in q_halves:
+            nc.vector.tensor_copy(
+                out=q_bf[:, rows, :].rearrange("p (c i) t -> p c t i", i=4),
+                in_=q_raw[:, :, rows].rearrange("p t (c i) -> p c t i", i=4),
+            )
+        for rows in q_halves:
+            nc.vector.quantize_mx(
+                out=q_codes[:, rows].bitcast(FP8X4),
+                scales=q_scales[:, rows],
+                in_=q_bf[:, rows, :].rearrange("p q t -> p (q t)"),
+            )
+
+        old_sb = sb.tile([P, T], F32, name="old_sb", tag="staged", align_bytes=64)
+        nc.sync.dma_start(out=old_sb[:], in_=old)
 
         a = sb.tile([P, T], F32, name="a")
-        for n in range(T // N_TILE):
-            cols = slice(n * N_TILE, (n + 1) * N_TILE)
-            bank = psum.tile([P, N_TILE], F32, name="bank%d" % n)
+        starts = [sum(WIDTHS[:n]) for n in range(len(WIDTHS))]
+        for n, (c0, width) in enumerate(zip(starts, WIDTHS)):
+            cols = slice(c0, c0 + width)
+            bank = psum.tile([P, width], F32, name="bank%d" % n)
             nc.tensor.matmul_mx(
                 out=bank[:],
                 lhsT=q_codes[:].bitcast(FP8X4),
                 lhsT_scale=q_scales[:],
-                rhs=k_words[:, 2 * n * N_TILE : 2 * (n + 1) * N_TILE].bitcast(FP4X4),
+                rhs=k_words[:, 2 * c0 : 2 * (c0 + width)].bitcast(FP4X4),
                 rhs_scale=k_scales[:, cols],
                 start=True,
                 stop=True,

@@ -110,6 +110,8 @@ def tile_attend_difference_lean_throughtimes_heads_kernel(tc, query, keys_words,
         y = [sb.tile([P, HALF], F32, name="y%d" % h) for h in range(2)]
         nc.scalar.activation(picked[:], f2[:].indirect(list3[:, halves[1]]), COPY)
         nc.vector.tensor_tensor(y[0][:], f2[:].indirect(list3[:, halves[0]]), w[0][:], MULT)
-        nc.sync.dma_start(out=out[:, :HALF], in_=y[0][:])
-        nc.vector.tensor_tensor(y[1][:], picked[:], w[1][:], MULT)
-        nc.scalar.dma_start(out=out[:, HALF:], in_=y[1][:])
+        nc.scalar.dma_start(out=out[:, :HALF], in_=y[0][:])
+        for c0, queue in ((0, nc.scalar), (HALF // 2, nc.sync)):
+            cols = slice(c0, c0 + HALF // 2)
+            nc.vector.tensor_tensor(y[1][:, cols], picked[:, cols], w[1][:, cols], MULT)
+            queue.dma_start(out=out[:, HALF + c0 : HALF + c0 + HALF // 2], in_=y[1][:, cols])

from contextlib import ExitStack

import concourse.mybir as mybir

D, T, I, Q = 512, 1024, 512, 128
FLOPS = 2 * D * T * Q

F32 = mybir.dt.float32
BF16 = mybir.dt.bfloat16
I32 = mybir.dt.int32
U32 = mybir.dt.uint32
U16 = mybir.dt.uint16
U8 = mybir.dt.uint8
FP8X4 = mybir.dt.float8_e4m3fn_x4
FP4X4 = mybir.dt.float4_e2m1fn_x4
ADD = mybir.AluOpType.add
MULT = mybir.AluOpType.mult
COPY = mybir.ActivationFunctionType.Copy

P = 128
PACK = 4
WIDTHS = (256, 256, 256, 128, 128)
HALF = I // 2
LIST_COLS = I // 16
HALF_COLS = LIST_COLS // 2


def tile_attend_difference_lean_throughtimes_heads_kernel(tc, query, keys_words, keys_scales, old, offs, offs2, offs3, out):
    nc = tc.nc
    with ExitStack() as ctx:
        sb = ctx.enter_context(tc.tile_pool(name="sb", bufs=1))
        psum = ctx.enter_context(tc.psum_pool(name="psum", bufs=1))

        list1 = sb.tile([P, LIST_COLS], U16, name="list1")
        list2 = sb.tile([P, LIST_COLS], U16, name="list2")
        list3 = sb.tile([P, LIST_COLS], U16, name="list3")
        q_raw = sb.tile([P, PACK, Q], F32, name="q_raw", tag="staged", align_bytes=64)
        k_words = sb.tile([P, 2 * T], U8, name="k_words", align_bytes=64)
        k_scales = sb.tile([P, T], U8, name="k_scales", align_bytes=64)
        f1 = sb.tile([P, T], F32, name="f1")

        nc.vector.memset(k_scales[:].bitcast(U32), 0)
        nc.sync.dma_start(out=q_raw[:], in_=query.rearrange("(p j) q -> p j q", j=PACK))
        nc.sync.dma_start(out=k_words[:].bitcast(I32), in_=keys_words[0].bitcast(I32))
        for quad in range(4):
            (nc.sync if quad < 2 else nc.scalar).dma_start(
                out=k_scales[32 * quad : 32 * quad + 4, :].bitcast(I32),
                in_=keys_scales[0, 4 * quad : 4 * quad + 4, :].bitcast(I32),
            )
        nc.sync.dma_start(list1[:], offs)
        nc.sync.dma_start(list2[:], offs2)
        nc.sync.dma_start(list3[:], offs3)
        nc.vector.memset(f1[:], 0.0)

        q_bf = sb.tile([P, Q, PACK], BF16, name="q_bf", align_bytes=64)
        q_codes = sb.tile([P, Q], U32, name="q_codes", align_bytes=64)
        q_scales = sb.tile([P, Q], U8, name="q_scales", align_bytes=64)
        q_halves = [slice(0, Q // 2), slice(Q // 2, Q)]
        for rows in q_halves:
            nc.vector.tensor_copy(
                out=q_bf[:, rows, :].rearrange("p (c i) t -> p c t i", i=4),
                in_=q_raw[:, :, rows].rearrange("p t (c i) -> p c t i", i=4),
            )
        for rows in q_halves:
            nc.vector.quantize_mx(
                out=q_codes[:, rows].bitcast(FP8X4),
                scales=q_scales[:, rows],
                in_=q_bf[:, rows, :].rearrange("p q t -> p (q t)"),
            )

        old_sb = sb.tile([P, T], F32, name="old_sb", tag="staged", align_bytes=64)
        nc.sync.dma_start(out=old_sb[:], in_=old)

        a = sb.tile([P, T], F32, name="a")
        starts = [sum(WIDTHS[:n]) for n in range(len(WIDTHS))]
        for n, (c0, width) in enumerate(zip(starts, WIDTHS)):
            cols = slice(c0, c0 + width)
            bank = psum.tile([P, width], F32, name="bank%d" % n)
            nc.tensor.matmul_mx(
                out=bank[:],
                lhsT=q_codes[:].bitcast(FP8X4),
                lhsT_scale=q_scales[:],
                rhs=k_words[:, 2 * c0 : 2 * (c0 + width)].bitcast(FP4X4),
                rhs_scale=k_scales[:, cols],
                start=True,
                stop=True,
            )
            if n % 2 == 0:
                nc.scalar.activation(a[:, cols], bank[:], COPY)
            else:
                nc.vector.tensor_copy(a[:, cols], bank[:])

        halves = [slice(h * HALF_COLS, (h + 1) * HALF_COLS) for h in range(2)]
        plus = [sb.tile([P, HALF], F32, name="plus%d" % h) for h in range(2)]
        minus = [sb.tile([P, HALF], F32, name="minus%d" % h) for h in range(2)]
        w = [sb.tile([P, HALF], F32, name="w%d" % h) for h in range(2)]

        nc.vector.tensor_copy(plus[0][:], a[:].indirect(list1[:, halves[0]]))
        nc.scalar.activation(minus[0][:], a[:].indirect(list2[:, halves[0]]), COPY, scale=-1.0)
        nc.scalar.activation(plus[1][:], a[:].indirect(list1[:, halves[1]]), COPY)
        nc.scalar.activation(minus[1][:], a[:].indirect(list2[:, halves[1]]), COPY, scale=-1.0)
        for h in range(2):
            nc.vector.tensor_tensor(f1[:].indirect(list1[:, halves[h]]), plus[h][:], minus[h][:], ADD)
            nc.vector.tensor_tensor(w[h][:], plus[h][:], minus[h][:], ADD)

        f2 = sb.tile([P, T], F32, name="f2")
        nc.vector.tensor_tensor(f2[:], f1[:], old_sb[:], ADD)

        picked = sb.tile([P, HALF], F32, name="picked")
        y = [sb.tile([P, HALF], F32, name="y%d" % h) for h in range(2)]
        nc.scalar.activation(picked[:], f2[:].indirect(list3[:, halves[1]]), COPY)
        nc.vector.tensor_tensor(y[0][:], f2[:].indirect(list3[:, halves[0]]), w[0][:], MULT)
        nc.scalar.dma_start(out=out[:, :HALF], in_=y[0][:])
        for c0, queue in ((0, nc.scalar), (HALF // 2, nc.sync)):
            cols = slice(c0, c0 + HALF // 2)
            nc.vector.tensor_tensor(y[1][:, cols], picked[:, cols], w[1][:, cols], MULT)
            queue.dma_start(out=out[:, HALF + c0 : HALF + c0 + HALF // 2], in_=y[1][:, cols])
